import numpy as np, ml_dtypes
CORES = [23,119,17,113]
N = 4
import mx_ref
BF = ml_dtypes.bfloat16
def gentries(a):
    return np.ascontiguousarray(a.reshape(8, 16, -1).transpose(0, 2, 1)).reshape(8, -1)
def gtable(e):
    e = np.asarray(e); return np.ascontiguousarray(e.reshape(8, -1, 16).transpose(0, 2, 1)).reshape(128, -1).astype(np.int32)
def gcols(t, e):
    v = np.concatenate([t.reshape(8, 16, -1, 4), np.zeros((8, 16, 1, 4), BF)], axis=2)
    return np.ascontiguousarray(np.stack([v[g][:, e[g]] for g in range(8)])).reshape(128, -1)
def tile(rs):
    return np.stack(rs, axis=2).reshape(128, -1).astype(BF)
def pick(q, e):
    c = np.concatenate([q[0].reshape(128, -1, 4), np.zeros((128, 1, 4), np.uint8)], axis=1); s = np.concatenate([q[1], np.ones((16, 1), np.uint8)], axis=1)
    return (np.ascontiguousarray(c[:, e].reshape(128, -1)), np.ascontiguousarray(s[:, e]))
def join(*qs):
    return (np.concatenate([q[0] for q in qs], axis=1), np.concatenate([q[1] for q in qs], axis=1))
def put(q, e, v):
    c, s = q[0].reshape(128, -1, 4).copy(), q[1].copy(); c[:, e] = v[0].reshape(128, -1, 4); s[:, e] = v[1]
    return (c.reshape(128, -1), s)
def pk(c, s):
    return (np.ascontiguousarray(c), mx_ref.live(s))
def emit(q):
    return q[0], q[1]
def packed(v, rng):
    q = [mx_ref.quantize(np.ascontiguousarray(v[r])) for r in range(N)]
    return np.stack([a for a, b in q]), np.stack([mx_ref.plane(b, rng) for a, b in q])
def values_of_codes():
    e, c = np.zeros((128, 128, 4), np.float32), np.zeros((128, 2, 4), np.uint8)
    e[np.arange(128), np.arange(128), 0] = 1
    c[:127, :, 0] = np.arange(256).reshape(2, 128).T[:127]
    return mx_ref.matmul(mx_ref.quantize(e.reshape(128, 512).astype(BF)), (c.reshape(128, 8), np.full((16, 2), 127, np.uint8))).T.reshape(-1).astype(np.float64)
CODE_VALUE, SCALE_VALUE = values_of_codes(), 2.0 ** (np.arange(256) - 127.0)
def decode(q):
    return (CODE_VALUE[q[0]].reshape(16, 8, -1, 4) * SCALE_VALUE[q[1]][:, None, :, None] + 0.0).reshape(128, -1).astype(np.float32)
def f(rng, *shape):
    return mx_ref.flush((rng.standard_normal(shape, dtype=np.float32) * np.exp2(rng.integers(-2, 3, shape[:-1] + (1,)))).astype(BF))
def wide(rng, *shape, cols=0):
    v = rng.standard_normal(shape, dtype=np.float32) * np.exp2(rng.integers(-12, 13, shape)).astype(np.float32)
    if cols: v *= np.repeat(np.exp2(rng.integers(-cols, cols + 1, shape[:-2] + (1, shape[-1] // 4))) * (rng.random(shape[:-2] + (1, shape[-1] // 4)) > 0.0625), 4, axis=-1).astype(np.float32)
    return mx_ref.flush(v.astype(BF))
C, M, WIDTH = 384, 16, 24
ROUNDS = 3
def big(v):
    v = v.astype(np.float32)
    v[np.abs(v) < np.float32(2.0 ** -16)] = 0
    return v.astype(BF)
def numbers_of(rng):
    return {"x": np.array(f(rng, N, 128, 4 * C)), "u": np.array(f(rng, N, 128, 512)), "v": np.array(f(rng, N, 128, 512))}
def towers(rng):
    return np.stack([gtable(np.stack([rng.permutation(C) for g in range(8)])) for r in range(N)])
def layers(rng):
    w = f(rng, N, 128, 2048).astype(np.float32).reshape(N, 128, 512, 4)
    w[rng.random(w.shape) < 0.9375] = 0
    m = np.searchsorted(28.0 * 2.0 ** np.arange(-20.0, 30.0), np.sum(np.abs(w), axis=(1, 3), keepdims=True))
    return np.array(mx_ref.flush((w * (2.0 ** (20.0 - m)).astype(np.float32)).astype(BF))).astype(np.float32)
def mirror(k):
    w, i = np.zeros((N, 128, 4, 128, 4), np.float32), np.arange(128)
    for b in range(4): w[:, i, b, i, b] = 32 * k[:, None]
    return w.reshape(N, 128, 512, 4)
def weights(rng, w):
    c, s = packed(np.ascontiguousarray(w).reshape(N, 128, 2048).astype(BF), rng)
    return {"wc": c, "ws": s}
def setup_inputs(rng):
    return {**numbers_of(rng), "tw": towers(rng), **weights(rng, layers(rng))}
def setup_inputs_ties(rng):
    d = numbers_of(rng)
    x = d["x"].astype(np.float32).reshape(N, 8, 16, C, 4)
    x[:, :, :8] = 0
    x[:, :, 0, :, 0] = rng.integers(0, 4, (N, 8, C))
    n = (N, 8, 8, C, 4)
    a = (1 + (2 * rng.integers(0, 64, n) + 1) / 128) * np.exp2(rng.integers(-14, -7, n)) * rng.choice([-1.0, 1.0], n)
    a[:, :, 0, :, 0] = 1.96875
    x[:, :, 8:] = a * np.exp2(rng.integers(-2, 3, (N, 8, 1, 1, 1)))
    u = d["u"].reshape(N, 128, 128, 4)
    u[:, :, ::16] = 0
    o = rng.permutation(N)
    for r in range(N):
        for h in range(0, 128, 16): u[r, h, h, 0] = 0.0 if r == o[0] else -1.0 if r in (o[1], o[3]) else 1.0
    w = layers(rng)
    w.reshape(N, 128, 4, 8, 16, 4)[:, :, :, :, :8] = 0
    return {"x": x.reshape(N, 128, 4 * C).astype(BF), "u": u.reshape(N, 128, 512), "v": d["v"], "tw": towers(rng), **weights(rng, w)}
def setup_inputs_near(rng):
    d = numbers_of(rng)
    x = d["x"].astype(np.float32).reshape(N, 8, 16, C, 4)
    u = d["u"].reshape(N, 128, 128, 4)
    u[:, :, ::16] = 0
    x[:, :, 0] = 0
    x[:, :, 8:] = 0
    s = rng.integers(0, 16, (N, 8, C))
    o = rng.permutation(8) % 4
    turn = np.arange(N) % 2 == rng.integers(2)
    w = mirror(np.ones(N)).reshape(N, 128, 4, 128, 4)
    for g in range(8):
        h = 16 * g
        if o[g] < 3:
            k = 2.0 ** -30 if o[g] == 2 else 1.0
            x[:, g, 0, :, 0] = -1.0 if o[g] == 1 else 1.0
            x[:, g, 8] = ((s[:, g, :, None] >> np.arange(4)) & 1) * np.exp2(np.arange(4) - 23.0)
            x[:, g, 11, :, 0] = 2.0 ** -10
            u[:, h, h, 0] = k
            u[:, h + 8, h] = k
            u[:, h + 11, h, 0] = k
            if o[g] == 0:
                x[turn, g, 8] = 0
                u[turn, h + 8, h] = -4.0
        else:
            x[:, g, 9:11, :, 0] = (1 + rng.integers(0, 8, (N, 2, C)) / 8) * 2.0 ** -30
            x[:, g, 12, :, 0] = 2.0 ** -30
            u[:, h + 9, h, 0] = -2.0 ** -30
            u[:, h + 10, h, 0] = 1.125 * 2.0 ** -30
            x[turn, g, 9:11] = 0
            u[turn, h + 9, h, 0] = 2.0 ** -30
            u[turn, h + 10, h, 0] = -1.125 * 2.0 ** -30
            for i in (h + 9, h + 10): w[turn, i, :, i] *= np.float32(2.0 ** -9)
    far = rng.permutation(np.nonzero(o < 3)[0])[:4]
    for r in range(N):
        for g in far: x[r, g, 0, rng.integers(C), 0] = 2.0 ** 30 * rng.choice([-1.0, 1.0])
    return {"x": x.reshape(N, 128, 4 * C).astype(BF), "u": u.reshape(N, 128, 512), "v": d["v"], "tw": towers(rng), **weights(rng, w)}
def setup_inputs_huge(rng):
    d = numbers_of(rng)
    o = rng.permutation(N)
    c = rng.choice([-1.0, 1.0], N)
    x = (0.6 + 0.4 * rng.random((N, 128, C, 4))) * 2.0 ** 30 * c[:, None, None, None]
    x[o < N // 2] *= rng.choice([-1.0, 1.0], (N // 2, 1, C, 1))
    u = d["u"].astype(np.float32).reshape(N, 128, 128, 4)
    k = np.stack([rng.permutation(8) % 2 * 2.0 - 1.0 for r in range(N)])
    u[:, :, ::16] = 2.0 ** 30 * (1 - 0.1 * rng.random((N, 128, 8, 4))) * k[:, None, :, None]
    e = int(np.argmax(o))
    a = np.where(rng.random((128, C, 4)) < rng.random((1, C, 1)), 0.9375, 1.0)
    a[::8, :, 0] = 1.0
    x[e] = a * 2.0 ** 30 * c[e]
    u[e, :, ::16] = 2.0 ** 30 * k[e][None, :, None]
    return {"x": x.astype(np.float32).reshape(N, 128, 4 * C).astype(BF), "u": u.reshape(N, 128, 512).astype(BF), "v": d["v"], "tw": towers(rng), **weights(rng, mirror(c * np.roll(c, 1)))}
def setup_inputs_ends(rng):
    d = numbers_of(rng)
    s, k0 = rng.choice([-1.0, 1.0]), int(rng.integers(4))
    x = d["x"].astype(np.float32).reshape(N, 128, C, 4)
    u = d["u"].astype(np.float32).reshape(N, 128, 128, 4)
    w, m, p = layers(rng), mirror(np.ones(N)), []
    for r in range(N):
        k = (r + k0) % 4
        c = (rng.permutation(8) % 2 * 2.0 - 1.0)[None, :, None]
        e = np.stack([rng.permutation(C)] * 8)
        if k == 0:
            x[r], w[r], u[r, :, ::16] = s * 2.0 ** 30, 0.0, 2.0 ** 30 * c
            e[:] = np.arange(C)
        elif k == 1:
            x[r], w[r], u[r, :, ::16] = s * 2.0 ** -30, m[r], 2.0 ** -30 * c
            e[:] = np.arange(C)[::-1]
        elif k == 2:
            x[r] = 2.0 ** 30 * rng.choice([-1.0, 1.0], (1, C, 1))
            w[r] = 0.0625 * rng.choice([-1.0, 1.0], (1, 512, 1))
            u[r, :, ::16] = 2.0 ** 30 * c
        else:
            for g in range(8): e[g] = np.roll(np.arange(C), g)
        p.append(gtable(e))
    d["v"] = (np.where(d["v"] < 0, -1.0, 1.0) * np.where(rng.permutation(N) % 2, 2.0 ** -30, 2.0 ** 30)[:, None, None]).astype(np.float32).astype(BF)
    return {"x": x.reshape(N, 128, 4 * C).astype(BF), "u": u.reshape(N, 128, 512).astype(BF), "v": d["v"], "tw": np.stack(p), **weights(rng, w)}
def setup_inputs_spread(rng):
    d = setup_inputs(rng)
    d["x"] = big(wide(rng, N, 128, 4 * C, cols=4))
    return d
def check_inputs(d):
    b = []
    for k in ("x", "u", "v"):
        a = np.abs(d[k].astype(np.float32))
        if not (np.isfinite(a).all() and ((a == 0) | (a >= 2.0 ** -30) & (a <= 2.0 ** 30)).all()): b.append("a value of " + k)
    none, least, most = [emit(mx_ref.quantize(np.full((128, 16), k, np.float32).astype(BF)))[1][0, 0] for k in (0.0, 2.0 ** -30, 2.0 ** 30)]
    for r in range(N):
        if (np.sort(gentries(d["tw"][r]), axis=1) != np.arange(C)).any(): b.append("tw: a group's entries aren't a permutation")
        if ((d["wc"][r] == 0x7F) | (d["wc"][r] == 0xFF)).any(): b.append("wc: a code that is no number")
        s = mx_ref.live(d["ws"][r])
        if ((s != none) & ((s < least) | (s > most))).any(): b.append("ws: a scale out of range")
        elif not (np.sum(np.abs(decode(pk(d["wc"][r], d["ws"][r])).astype(np.float64)).reshape(128, 512, 4), axis=(0, 2)) <= 32).all(): b.append("W: the sizes of a column are beyond 32 together")
    return b
def reference(x, u, v, tw, wc, ws):
    qu = [mx_ref.quantize(u[r]) for r in range(N)]
    lay = [pk(wc[r], ws[r]) for r in range(N)]
    now = [x[r] for r in range(N)]
    base = [gentries(tw[r]).reshape(8, M, WIDTH) for r in range(N)]
    top = [gentries(tw[r]).reshape(8, M, WIDTH) for r in range(N)]
    up = np.zeros((N, 8, C), np.int64)
    for t in range(ROUNDS):
        h = WIDTH >> (t + 1)
        own, ends = [], []
        for r in range(N):
            q = mx_ref.quantize(now[r])
            s = mx_ref.matmul(qu[r], q)[::16] + np.float32(0.0)
            own.append(decode(q).astype(BF))
            score = np.take_along_axis(s, base[r].reshape(8, -1), axis=1).reshape(8, M, 2 * h)
            o = np.argsort(-score, axis=2, kind="stable")
            b, e = np.take_along_axis(base[r], o, axis=2), np.take_along_axis(top[r], o, axis=2)
            np.put_along_axis(up[r], e[:, :, :h].reshape(8, -1), np.roll(b[:, :, h:], 1, axis=1).reshape(8, -1), axis=1)
            base[r], top[r] = b[:, :, :h], np.roll(e[:, :, h:], 1, axis=1)
            np.put_along_axis(up[r], top[r].reshape(8, -1), np.stack([C + np.arange(M * h)] * 8), axis=1)
            a = gcols(own[r], top[r].reshape(8, -1)).astype(np.float32) + gcols(own[r], base[r].reshape(8, -1)).astype(np.float32)
            ends.append(mx_ref.quantize(np.ascontiguousarray((a * np.float32(0.5)).astype(BF))))
        for r in range(N):
            made = tile([mx_ref.matmul(pick(lay[r], np.arange(128 * b, 128 * b + 128)), ends[r - 1]) * np.float32(0.03125) for b in range(4)])
            near = gcols(np.concatenate([own[r], made], axis=1), up[r]).astype(np.float32)
            now[r] = ((own[r].astype(np.float32) + near) * np.float32(0.5)).astype(BF)
    y, op = np.zeros((N, 128, C), np.float32), np.zeros((N, 8, C), np.float32)
    oc, osc = np.zeros((N, 128, 4 * C), np.uint8), np.zeros((N, 16, C), np.uint8)
    for r in range(N):
        q = mx_ref.quantize(now[r])
        y[r] = mx_ref.matmul(mx_ref.quantize(v[r]), q)
        op[r] = up[r]
        oc[r], osc[r] = emit(q)
    return {"y": y, "op": op, "oc": oc, "osc": osc}

from concourse.mybir import dt, AluOpType, ActivationFunctionType

A = AluOpType
COPY = ActivationFunctionType.Copy
P = 384
LANES = {1: 24, 2: 12, 3: 6}
B0 = {1: 14, 2: 8, 3: 6}
NR = {1: 576, 2: 144, 3: 48}
NE = {1: 688, 2: 208, 3: 80}
SG0 = {1: 0, 2: 44, 3: 58}
VW = {1: 576, 2: 480, 3: 432}
XB = {1: "X1", 2: "X2", 3: "X3", 4: "X2"}
BF, F32, U16, I32, U8, FP8 = "bfloat16", "float32", "uint16", "int32", "uint8", "float8_e4m3fn_x4"

SCRATCH = {}


def _buf(name, cols, dtype, where="sbuf"):
    SCRATCH[name] = (where, [128, cols], dtype)


for _n, _c in (("QX1", P), ("QX2", P), ("QX3", P), ("QX4", P), ("QU", 128), ("UR", 128), ("QV", 128), ("WW", 512),
               ("EC", 512), ("LX", P), ("LE2", 224), ("LE3", 176), ("QE1", 192), ("QE2", 128), ("QE3", 128)):
    _buf(_n + "c", _c, FP8)
    _buf(_n + "s", _c, U8)
for _n, _c, _t in (
        ("X1", 4 * P, BF), ("X2", 4 * P, BF), ("X3", 4 * P, BF), ("ub", 512, BF), ("vb", 512, BF), ("half", 704, BF),
        ("zi", 516, BF), ("FP", 4 * P, BF), ("FQ", 960, BF), ("E1", 768, BF), ("E2", 512, BF), ("E3", 704, BF),
        ("tmp", 832, BF), ("tb", 576, BF), ("m16s", 16, BF), ("m16", P, BF), ("seg16", P, BF), ("C", 576, BF), ("CS", 576, BF),
        ("tw32", 24, I32), ("ic", 24, I32), ("mi", 16, I32), ("ui", 8, I32), ("ti", 96, I32),
        ("tw16", 24, U16), ("il", 24, U16), ("ul", 8, U16), ("LL", 26, U16), ("SL", 12, U16),
        ("US", 14, U16), ("BL", 24, U16), ("UL", 24, U16), ("SG", 64, U16),
        ("cols", 8, F32), ("iotaR", 576, F32), ("J", 44, F32), ("KK", 24, F32), ("fe", 24, F32), ("R", 96, F32),
        ("opc", 52, F32), ("UP", P, F32), ("ms", P, F32), ("ht", P, F32), ("ysb", P, F32),
        ("SS", P, F32), ("GM", P, F32), ("SC", P, F32), ("BX", 576, F32), ("M", 688, F32), ("HS", 688, F32),
        ("tf", 448, F32), ("sl", 32, F32), ("DB", 28, F32), ("VB", 208, F32), ("tbB", 24, F32), ("tbT", 12, F32)):
    _buf(_n, _c, _t)
for _r in (1, 2, 3):
    _h = LANES[_r] // 2
    for _n, _c, _t in (("V", 4 * VW[_r], BF), ("D0", NR[_r], BF), ("DS", NE[_r], BF), ("KA", 64, F32), ("T", NE[_r], F32),
                       ("D", 28, F32), ("CL", B0[_r] + _h, U16),
                       ("MN", NR[_r] // 16, U16), ("MX", NR[_r] // 16, U16), ("KL", NE[_r] // 16, U16)):
        _buf(_n + str(_r), _c, _t)
for _i in range(8):
    _buf("p%d" % _i, 512, F32, "psum")

NDMA = 26
SEMAPHORES = ["vs", "ss", "ts", "gs", "loc", "axc", "axs", "all1", "a2c", "a2s", "a3c", "a3s"] + ["d%d" % i for i in range(NDMA)]


def rank_program(g, core, T, topo):
    rank = T.rank_of(core)
    if rank is None:
        return
    nxt = T.cores[(rank + 1) % len(T.cores)]
    rid, pid = topo.addr(nxt)[:2]
    mask = topo.mask(core, nxt)
    neng = len(topo.engines(core, nxt))

    ENG = {"v": g.vector, "s": g.scalar, "t": g.tensor, "g": g, "y": g.sync}
    QSEM = {"v": "vs", "s": "ss", "t": "ts", "g": "gs"}
    cnt, known, wr, rd, nd = {}, {q: {} for q in ENG}, {}, {}, [0]

    def before(q, reads, writes):
        ev = []
        for k in reads:
            ev += wr.get(k, [])
        for k in writes:
            ev += wr.get(k, []) + rd.get(k, [])
        for sem, val, clock in sorted(ev, key=lambda e: -e[1]):
            if known[q].get(sem, 0) < val:
                ENG[q].wait_ge(T.sem[sem], val)
                for k2, v2 in clock.items():
                    if known[q].get(k2, 0) < v2:
                        known[q][k2] = v2

    def after(q, sem, reads, writes):
        clock = dict(known[q])
        clock[sem] = cnt[sem]
        ev = (sem, cnt[sem], clock)
        for k in reads:
            rd.setdefault(k, []).append(ev)
        for k in writes:
            wr[k] = [ev]
            rd[k] = []

    def op(q, reads, writes, fn):
        before(q, reads, writes)
        sem = QSEM[q]
        fn().then_inc(T.sem[sem], 1)
        cnt[sem] = cnt.get(sem, 0) + 1
        after(q, sem, reads, writes)

    def dma(q, out, in_, reads, writes):
        before(q, reads, writes)
        sem = "d%d" % nd[0]
        nd[0] += 1
        ENG[q].dma_start(out, in_).then_inc(T.sem[sem], 16)
        cnt[sem] = 16
        after(q, sem, reads, writes)

    def send(out, in_, sem, reads, lands):
        before("g", reads, [])
        g.remote_dma(out, in_, T.sem[sem], T.sem.loc, pid, rid, mask)
        cnt["loc"] = cnt.get("loc", 0) + neng
        cnt[sem] = neng
        wr[lands] = wr.get(lands, []) + [(sem, neng, {sem: neng})]

    def ts(out, w, in0, rds, s1, op0, s2=None, op1=None):
        if op1 is None:
            op("v", rds, [w], lambda: g.vector.tensor_scalar(out, in0, s1, None, op0))
        else:
            op("v", rds, [w], lambda: g.vector.tensor_scalar(out, in0, s1, s2, op0, op1))

    def tt(out, w, in0, in1, rds, o):
        op("v", rds, [w], lambda: g.vector.tensor_tensor(out, in0, in1, o))

    def vcopy(out, w, in_, rds):
        op("v", rds, [w], lambda: g.vector.tensor_copy(out, in_))

    def memset(out, w, k):
        op("v", [], [w], lambda: g.vector.memset(out, k))

    def scan(out, w, d0, d1, rds, o0, o1):
        op("v", rds, [w], lambda: g.vector.tensor_tensor_scan(out, d0, d1, 0.0, o0, o1))

    def act(out, w, in_, rds, scale=None):
        if scale is None:
            op("s", rds, [w], lambda: g.scalar.activation(out, in_, COPY))
        else:
            op("s", rds, [w], lambda: g.scalar.activation(out, in_, COPY, scale=scale))

    def fill(out, w, n, value):
        act(out, w, T.half[:, 0:n], ["half"], scale=2.0 * value)

    def quant(qc, qs, w, in_, rds):
        op("v", rds, [w], lambda: g.vector.quantize_mx(qc, qs, in_))

    def mm(bank, n, lc, ls, rc, rs, rds):
        op("t", rds, ["p%d" % bank], lambda: g.tensor.matmul_mx(T["p%d" % bank][:, 0:n], lc, ls, rc, rs, True, True))

    def iota(out, w, pattern, base, cm, flt=True):
        if flt:
            op("g", [], [w], lambda: g.iota(out, pattern, base, cm, allow_small_or_imprecise_dtypes=True))
        else:
            op("g", [], [w], lambda: g.iota(out, pattern, base, cm))

    col = {k2: T.cols[:, i:i + 1] for i, k2 in enumerate(("i", "m0", "n0", "m15", "n15", "p4"))}

    dma("s", T.tw32[:], T.tw[:, :], [], ["tw32"])
    for c in range(3):
        dma("y", T.X1[:, 512 * c:512 * c + 512], T.x[:, 512 * c:512 * c + 512], [], ["X1%d" % c])
    dma("s", T.ub[:], T.u[:, :], [], ["ub"])
    dma("y", T.WWc[:].bitcast(dt.uint8), T.wc[:, :], [], ["WWc"])
    dma("y", T.WWs[:], T.ws[:, :], [], ["WWs"])
    dma("y", T.vb[:], T.v[:, :], [], ["vb"])

    iota(T.ic[:], "ic", [[0, 24]], 0, 1, False)
    iota(T.J[:], "J", [[16, 44]], 0, 0)
    iota(T.mi[:], "mi", [[1, 16]], 128, -1, False)
    iota(T.iotaR[:], "iotaR", [[1, 576]], 0, 0)
    iota(T.ui[:], "ui", [[16, 8]], 0, 0, False)
    iota(T.KK[:], "KK", [[-1, 24]], 22, 0)
    for r in (1, 2, 3):
        iota(T.R[:, 32 * r - 32:32 * r - 32 + B0[r]], "Ra%d" % r, [[1, B0[r]]], 0, 0)
        iota(T.R[:, 32 * r - 32 + B0[r]:32 * r], "Rb%d" % r, [[1, 32 - B0[r]]], LANES[r] // 2, 0)

    ts(col["p4"], "p4", T.ic[:, 0:1], ["ic"], 4.0, A.mult, 3.0, A.add)
    ts(T.ic[:], "ic", T.ic[:], ["ic"], 15, A.bitwise_and)
    ts(T.mi[:], "mi", T.mi[:], ["mi"], 15, A.bitwise_and)
    ts(col["i"], "ci", T.ic[:, 0:1], ["ic"], 1.0, A.mult)
    vcopy(T.il[:], "il", T.ic[:], ["ic"])
    ts(T.m16s[:], "m16s", T.mi[:], ["mi"], 0.0, A.is_equal)
    ts(T.J[:], "J", T.J[:], ["J", "ci"], col["i"], A.add)
    memset(T.half[:], "half", 0.5)
    for k2, val, o in (("m0", 0.0, A.is_equal), ("n0", 0.0, A.not_equal), ("m15", 15.0, A.is_equal), ("n15", 15.0, A.not_equal)):
        ts(col[k2], k2, T.ic[:, 0:1], ["ic"], val, o)

    def pair_lists(r):
        W, n = LANES[r], NR[r] // 16
        j = T.J[:, 0:n]
        k, kw, kp, mn, mx = T.ti[:, 0:n], T.tf[:, 0:n], T.tf[:, 48:48 + n], T.tf[:, 96:96 + n], T.tf[:, 144:144 + n]
        ts(k, "k", j, ["J"], 1.0 / W, A.mult, -(W - 1) / (2.0 * W), A.add)
        yield
        ts(kw, "kw", k, ["k"], -float(W), A.mult)
        yield
        tt(kp, "kp", j, kw, ["J", "kw"], A.add)
        yield
        tt(mn, "mn", k, kp, ["k", "kp"], A.min)
        tt(mx, "mx", k, kp, ["k", "kp"], A.max)
        yield
        ts(T["MX%d" % r][:], "MX%d" % r, mx, ["mx"], 16.0, A.mult, 15.0, A.add)
        ts(T["MN%d" % r][:], "MN%d" % r, mn, ["mn"], 16.0, A.mult, 15.0, A.add)
        yield

    def key_lists(r):
        n, L, b0 = NE[r] // 16, LANES[r] + 1, B0[r]
        j = T.J[:, 0:n]
        sg, sl, ps, ad = T.ti[:, 48:48 + n], T.tf[:, 192:192 + n], T.tf[:, 256:256 + n], T.tf[:, 320:320 + n]
        ts(sg, "sg", j, ["J"], 1.0 / L, A.mult, -(L - 1) / (2.0 * L), A.add)
        yield
        ts(sl, "slv", sg, ["sg"], -float(L), A.mult)
        vcopy(T.SG[:, SG0[r]:SG0[r] + n], "SG%d" % r, sg, ["sg"])
        yield
        tt(ps, "psv", j, sl, ["J", "slv"], A.add)
        yield
        if r == 1:
            vcopy(T.KL1[:], "KL1", ps, ["psv"])
        else:
            ts(ad, "adv", j, ["J"], float(b0 * L), A.is_ge, float(L), A.mult)
            yield
            tt(sl, "slv", ps, ad, ["psv", "adv"], A.add)
            yield
            vcopy(T["KL%d" % r][:], "KL%d" % r, sl, ["slv"])
        yield

    def thresholds(r):
        W = LANES[r]
        L, b0, n = W + 1, B0[r], NE[r]
        ns = b0 + W // 2 + 1
        t, R, a, b = T["T%d" % r], T.R[:, 32 * r - 32:32 * r], "Ra%d" % r, "Rb%d" % r
        ts(R[:, 0:b0], a, R[:, 0:b0], [a, "m0"], col["m0"], A.subtract, 0.0, A.max)
        yield
        u = T.tf[:, 416:416 + ns]
        ts(u, "uv", R[:, 0:ns], [a, b], 0.5, A.mult, -(W - 0.5), A.add)
        yield
        act(t[:], "T%d" % r, R.indirect(T.SG[:, SG0[r]:SG0[r] + n // 16]), [a, b, "SG%d" % r])
        yield
        yield
        yield
        tt(t[:, W:ns * L:L], "T%d" % r, R[:, 0:ns], u, [a, b, "uv"], A.mult)
        yield

    def together(*gens):
        gens = list(gens)
        while gens:
            gens = [x for x in gens if next(x, 1) is None]
            yield

    def signs(r):
        W, d, k = LANES[r], T["D0%d" % r], "D0%d" % r
        fill(d[:], k, NR[r], 1.0)
        fill(d[:, 0:W * W:W], k, W, 0.0)
        fill(d[:, 1:(W + 1) * (W - 2) + 2:W + 1], k, W - 1, -1.0)
        fill(d[:, W * W - 1:W * W], k, 1, -1.0)

    def resets(r):
        W = LANES[r]
        L, ns = W + 1, B0[r] + W // 2 + 1
        e, k = T["DS%d" % r], "DS%d" % r
        fill(e[:], k, NE[r], 1.0)
        if r == 1:
            fill(T.KA1[:, 24:25], "KA1z", 1, 1e6)
        else:
            fill(T["KA%d" % r][:, W:2 * W + 2:L], "KA%dz" % r, 2, 1e6)
            fill(T["KA%d" % r][:, 32 + W:32 + 2 * W + 2:L], "KB%dz" % r, 2, 1e6)
        fill(e[:, 0:ns * L:L], k, ns, 0.0)

    for _ in together(pair_lists(1), key_lists(1)):
        pass
    vcopy(T.ul[:], "ul", T.ui[:], ["ui"])
    vcopy(T.tw16[:], "tw16", T.tw32[:], ["tw32"])
    ts(T.zi[:], "zi", T.iotaR[:, 0:516], ["iotaR", "p4"], col["p4"], A.is_equal, 0.5, A.mult)

    act(T.m16[:], "m16", T.m16s[:, 0:16].indirect(T.il[:, 0:24]), ["m16s", "il"])
    fill(T.seg16[:], "seg16", P, 1.0)
    fill(T.KK[:, 23:24], "KK", 1, 1.0)
    fill(T.seg16[:, 0:P:16], "seg16", 24, 0.0)
    act(T.ms[:], "ms", T.iotaR[:, 0:P].indirect(T.tw16[:, 0:24]), ["iotaR", "tw16"])
    dma("y", T.fe[:, :], T.ms[0:128:16, :], ["ms"], ["fe"])

    CH = {1: [(0, 128), (128, 128), (256, 128)], 2: [(0, 256), (256, 128)], 3: [(0, 256), (256, 128)], 4: [(0, 192), (192, 192)]}
    QK = {r: ["QX%d%d" % (r, i) for i in range(len(CH[r]))] for r in CH}
    SK = {r: ["SS%d" % i for i in range(len(CH[r]))] for r in CH}

    def quant_x(r):
        for i, (a, n) in enumerate(CH[r]):
            quant(T["QX%dc" % r][:, a:a + n], T["QX%ds" % r][:, a:a + n], QK[r][i], T[XB[r]][:, 4 * a:4 * (a + n)],
                  ["X1%d" % i] if r == 1 else [XB[r] + "t%d" % t for t in range(5)])

    def score_products(r):
        for i, (a, n) in enumerate(CH[r]):
            mm(4 + i, n, T.URc[:], T.URs[:], T["QX%dc" % r][:, a:a + n], T["QX%ds" % r][:, a:a + n], ["URc", "URs", QK[r][i]])

    def unpack_products(qc, qs, banks, rds):
        for b in range(4):
            mm(banks[b], P, T.ECc[:, 128 * b:128 * b + 128], T.ECs[:, 128 * b:128 * b + 128], qc, qs, ["EC%d" % b] + rds)

    def plane(r, t):
        return T["V%d" % r][:, VW[r] * t:VW[r] * t + P]

    def own_plane(r, t):
        act(plane(r, t), "F%d%d" % (r, t), T["p%d" % t][:, 0:P], ["p%d" % t])

    def second_planes():
        for t, e in ((0, P), (1, P), (2, 192)):
            act(T.FQ[:, P * t:P * t + e], "FQ%d" % t, T["p%d" % t][:, 0:e], ["p%d" % t])

    def sort_keys(r, tbls, meanwhile):
        W = LANES[r]
        n16, n = 16 * W, NR[r]
        tt(T.GM[:, 0:n16], "GM", T.SS[:].indirect(T.BL[:, 0:W]), T.m16[:, 0:n16], SK[r] + ["BL", "m16"], A.mult)
        scan(T.SC[:, 0:n16], "SC", T.seg16[:, 0:n16], T.GM[:, 0:n16], ["seg16", "GM"], A.mult, A.add)
        mn, mx, mnk, mxk = T["MN%d" % r], T["MX%d" % r], "MN%d" % r, "MX%d" % r
        cuts = [(0, n)] if r > 1 else [(0, 192), (192, 384), (384, 576)]
        for a, b in cuts:
            lst = mx[:, a // 16:b // 16]
            if r == 1:
                act(T.BX[:, a:b], "BX%d" % a, T.SC[:].indirect(lst), ["SC", mxk])
            else:
                vcopy(T.BX[:, a:b], "BX%d" % a, T.SC[:].indirect(lst), ["SC", mxk])
        meanwhile()
        for a, b in cuts:
            tt(T.C[:, a:b], "C%d" % a, T.SC[:].indirect(mn[:, a // 16:b // 16]), T.BX[:, a:b], ["SC", mnk, "BX%d" % a], A.is_ge)
        scan(T.CS[:, 0:n], "CS", T["D0%d" % r][:], T.C[:, 0:n], ["D0%d" % r] + ["C%d" % a for a, b in cuts], A.mult, A.add)
        add_keys(r, 0, "KA", tbls)

    def add_keys(r, a, nm, tbls):
        W = LANES[r]
        for i, (tb, key) in enumerate(tbls):
            c = a + i * (W + 1)
            tt(T["KA%d" % r][:, c:c + W], "%s%d%d" % (nm, r, i), tb, T.CS[:, W - 1:W * W:W], [key, "CS"], A.subtract)

    def extract(r, a, nm, d, dk):
        W = LANES[r]
        L, n = W + 1, NE[r]
        ns = B0[r] + W // 2 + 1
        width = 25 if r == 1 else 2 * L
        rds = ["%s%d%d" % (nm, r, i) for i in range(1 if r == 1 else 2)] + ["%s%dz" % (nm, r)]
        tt(T.M[:, 0:n], "M", T["KA%d" % r][:, a:a + width].indirect(T["KL%d" % r][:]), T["T%d" % r][:],
           rds + ["KL%d" % r, "T%d" % r], A.min)
        scan(T.HS[:, 0:n], "HS", T["DS%d" % r][:], T.M[:, 0:n], ["DS%d" % r, "M"], A.mult, A.add)
        tt(d[:, 0:ns - 1], dk, T.HS[:, 2 * L - 1:ns * L:L], T.HS[:, L - 1:(ns - 1) * L:L], ["HS"], A.subtract)

    def first_lists(r):
        d, dk = T["D%d" % r], "D%d" % r
        extract(r, 0, "KA", d, dk)
        ts(T["CL%d" % r][:], "CL%d" % r, d[:, 0:B0[r] + LANES[r] // 2], [dk], 1024.0, A.mult, 383.0, A.min)

    def select(out, w, a0, a1, m, n, rds, t1, t2):
        ts(t1, "sel1" + w, a0, rds + [n], col[n], A.mult)
        ts(t2, "sel2" + w, a1, rds + [m], col[m], A.mult)
        tt(out, w, t1, t2, ["sel1" + w, "sel2" + w], A.add)

    def lower(r, d, dk, out, w):
        h = LANES[r] // 2
        select(out, w, d[:, 0:h], d[:, 1:h + 1], "m0", "n0", [dk], T.tf[:, 352:352 + h], T.tf[:, 366:366 + h])

    def upper_bases(r, d, dk, dz):
        h, a = LANES[r] // 2, B0[r]
        select(T.sl[:, 0:h + 1], "us", d[:, a - 1:a + h], d[:, a:a + h + 1], "m15", "n15", [dk, dz],
               T.tf[:, 380:380 + h + 1], T.tf[:, 394:394 + h + 1])
        ts(T.US[:, 0:h + 1], "US", T.sl[:, 0:h + 1], ["us"], 1024.0, A.mult, 383.0, A.min)

    def rows_of_bases(r):
        h = LANES[r] // 2
        act(T.VB[:, 0:16 * (h + 1)], "VB", T.iotaR[:, 0:P].indirect(T.US[:, 0:h + 1]), ["iotaR", "US"])

    def scatter_tops(r):
        h, b0 = LANES[r] // 2, B0[r]
        op("v", ["CL%d" % r, "iotaR"], ["UP"],
           lambda: g.vector.tensor_copy(T.UP[:].indirect(T["CL%d" % r][:, b0:b0 + h]), T.iotaR[:, P:P + 16 * h]))

    def scatter_links(r, low, lowk):
        op("v", [lowk, "VB"], ["UP"], lambda: g.vector.tensor_copy(T.UP[:].indirect(low), T.VB[:, 15:15 + 8 * LANES[r]]))

    def mask_up():
        scan(T.ms[:], "ms", T.UP[:], T.m16[:], ["UP", "m16"], A.add, A.mult)

    def blend_list():
        scan(T.ht[:], "ht", T.seg16[:], T.ms[:], ["seg16", "ms"], A.mult, A.add)
        vcopy(T.UL[:], "UL", T.ht[:, 15:P:16], ["ht"])

    def shift_tops(r):
        h, b0 = LANES[r] // 2, B0[r]
        d, dk = T["D%d" % r], "D%d" % r
        dma("y", T.tbT[1:128, 0:h], d[0:127, b0:b0 + h], [dk], ["tbT"])
        dma("y", T.tbT[0:128:16, 0:h], d[15:128:16, b0:b0 + h], [dk], ["tbT"])

    def make_e(r, win, wkeys, lst, lkey, meanwhile):
        h, b0 = LANES[r] // 2, B0[r]
        n = 16 * (h + 1)
        for t in range(4):
            act(T.tmp[:, n * t:n * t + n], "tmp%d" % t, win(t).indirect(lst[:, 0:h + 1]), [wkeys[t], lkey])
        second_planes()
        meanwhile()
        for t in range(4):
            tt(T["E%d" % r][:, t:64 * h:4], "E%d%d" % (r, t), win(t).indirect(lst[:, b0:b0 + h]),
               T.tmp[:, n * t + 1:n * t + 1 + 16 * h], [wkeys[t], lkey, "tmp%d" % t], A.add)

    def layer(r, ec, es, ekeys, n):
        h, w, v = LANES[r] // 2, VW[r], T["V%d" % r]
        for b in range(4):
            mm(4 + b, n, T.WWc[:, 128 * b:128 * b + 128], T.WWs[:, 128 * b:128 * b + 128], ec, es, ["WWc", "WWs"] + ekeys)
        for b in range(4):
            act(v[:, w * b + P:w * b + P + 16 * h], "H%d%d" % (r, b), T["p%d" % (4 + b)][:, 0:16 * h], ["p%d" % (4 + b)], scale=0.015625)

    def blend(r):
        h, w = LANES[r] // 2, VW[r]
        v, xn, xk = T["V%d" % r], T[XB[r + 1]], XB[r + 1]

        def near(t, a, b):
            return v[:, w * t:w * t + P + 16 * h].indirect(T.UL[:, a // 16:b // 16])

        def keys(t):
            return ["F%d%d" % (r, t), "H%d%d" % (r, t), "UL"]
        act(T.tb[:, 0:P], "tb0", near(3, 0, P), keys(3))
        act(T.tb[:, P:576], "tb1", near(2, 192, P), keys(2))
        for t, e in ((0, P), (1, P), (2, 192)):
            tt(xn[:, t:4 * e:4], xk + "t%d" % t, near(t, 0, e), T.FQ[:, P * t:P * t + e], keys(t) + ["FQ%d" % t], A.add)
        tt(xn[:, 3:4 * P:4], xk + "t3", T.tb[:, 0:P], T.p3[:, 0:P], ["tb0", "p3"], A.add)
        tt(xn[:, 770:4 * P:4], xk + "t4", T.tb[:, P:576], T.p2[:, 192:P], ["tb1", "p2"], A.add)

    def later_pads():
        memset(T.E2[:, 384:512], "E2z", 0.0)
        memset(T.E3[:, 192:704], "E3z", 0.0)
        quant(T.LE2c[:, 96:224], T.LE2s[:, 96:224], "LE2z", T.E3[:, 192:704], ["E3z"])
        quant(T.LE3c[:, 48:176], T.LE3s[:, 48:176], "LE3z", T.E3[:, 192:704], ["E3z"])

    f1, f2, f2t = thresholds(1), together(pair_lists(2), key_lists(2)), thresholds(2)
    f3 = together(pair_lists(3), key_lists(3), thresholds(3))

    def pump(f, n=99):
        for _ in range(n):
            if next(f, 1) is not None:
                break

    quant_x(1)
    quant(T.QUc[:], T.QUs[:], "QU", T.ub[:], ["ub"])
    vcopy(T.URc[:].bitcast(dt.uint32), "URc", T.QUc[:].bitcast(dt.uint32).indirect(T.ul[:, 0:8]), ["QU", "ul"])
    act(T.URs[:], "URs", T.QUs[:].indirect(T.ul[:, 0:8]), ["QU", "ul"])
    send(T.LXc[:].bitcast(dt.uint8), T.QX1c[:].bitcast(dt.uint8), "axc", QK[1], "LX")
    send(T.LXs[:], T.QX1s[:], "axs", QK[1], "LX")
    score_products(1)
    for i, (a, n) in enumerate(CH[1]):
        act(T.SS[:, a:a + n], "SS%d" % i, T["p%d" % (4 + i)][:, 0:n], ["p%d" % (4 + i)])
    pump(f1, 3)
    signs(1)
    for b in range(4):
        quant(T.ECc[:, 128 * b:128 * b + 128], T.ECs[:, 128 * b:128 * b + 128], "EC%d" % b, T.zi[:, 3 - b:515 - b], ["zi"])
    unpack_products(T.QX1c[:], T.QX1s[:], (0, 1, 2, 3), QK[1])
    later_pads()
    ts(T.sl[:, 0:24], "us", T.fe[:], ["fe"], 1.0 / 1024, A.mult)
    vcopy(T.BL[:], "BL", T.fe[:], ["fe"])
    tt(T.tbB[:], "tbB", T.sl[:, 0:24], T.KK[:], ["us", "KK"], A.add)

    def r1_gap():
        pump(f1)
        pump(f2, 2)
        resets(1)
        pump(f2t, 3)
    sort_keys(1, [(T.tbB[:], "tbB")], r1_gap)
    for t in range(4):
        own_plane(1, t)
    first_lists(1)
    send(T.LL[:], T.CL1[:], "all1", ["CL1"], "LL")

    fill(T.D1[:, 26:27], "Dz1", 1, 0.0)
    fill(T.DB[:, 14:15], "DBz2", 1, 0.0)
    iota(T.opc[:, 0:48], "opc", [[1, 3], [3, 16]], P + 3, 0)
    iota(T.opc[:, 48:51], "opf", [[1, 3]], P, 0)
    unpack_products(T.LXc[:], T.LXs[:], (4, 5, 6, 7), ["LX"])
    upper_bases(1, T.D1, "D1", "Dz1")
    scatter_tops(1)
    for t in range(4):
        act(T.FP[:, P * t:P * t + P], "FP%d" % t, T["p%d" % (4 + t)][:, 0:P], ["p%d" % (4 + t)])
        if t == 1:
            rows_of_bases(1)
    lower(1, T.D1, "D1", T.tbB[:, 0:12], "tbB")
    ts(T.BL[:, 0:12], "BL", T.tbB[:, 0:12], ["tbB"], 1024.0, A.mult)
    tt(T.tbB[:, 0:12], "tbB", T.tbB[:, 0:12], T.KK[:, 12:24], ["tbB", "KK"], A.add)
    pump(f2)
    pump(f2t)
    scatter_links(1, T.BL[:, 0:12], "BL")
    shift_tops(1)
    make_e(1, lambda t: T.FP[:, P * t:P * t + P], ["FP%d" % t for t in range(4)], T.LL, "LL", mask_up)
    quant(T.QE1c[:], T.QE1s[:], "QE1", T.E1[:], ["E1%d" % t for t in range(4)])
    layer(1, T.QE1c[:], T.QE1s[:], ["QE1"], 192)
    blend_list()
    blend(1)

    for r in (2, 3):
        W = LANES[r]
        h, b0 = W // 2, B0[r]
        n = 16 * h
        tbB, tbT = T.tbB[:, 0:W], T.tbT[:, 0:W]
        quant_x(r)
        score_products(r)
        unpack_products(T["QX%dc" % r][:], T["QX%ds" % r][:], (0, 1, 2, 3), QK[r])
        if r == 2:
            signs(2)
            resets(2)
        tt(tbT, "tbT", tbT, T.KK[:, 24 - W:24], ["tbT", "KK"], A.add)
        vcopy(T.SS[:, 0:256], "SS0", T.p4[:, 0:256], ["p4"])
        act(T.SS[:, 256:P], "SS1", T.p5[:, 0:128], ["p5"])
        for t in range(4):
            own_plane(r, t)
        if r == 2:
            signs(3)
            resets(3)
        sort_keys(r, [(tbB, "tbB"), (tbT, "tbT")], lambda: None)
        first_lists(r)

        def e_gap():
            add_keys(r, 32, "KB", [(tbT, "tbT"), (tbB, "tbB")])
        make_e(r, lambda t: plane(r, t), ["F%d%d" % (r, t) for t in range(4)], T["CL%d" % r], "CL%d" % r, e_gap)
        quant(T["QE%dc" % r][:], T["QE%ds" % r][:], "QE%d" % r, T["E%d" % r][:, 0:512], ["E%d%d" % (r, t) for t in range(4)] + ["E%dz" % r])
        send(T["LE%dc" % r][:, 0:n].bitcast(dt.uint8), T["QE%dc" % r][:, 0:n].bitcast(dt.uint8), "a%dc" % r, ["QE%d" % r], "LE%d" % r)
        send(T["LE%ds" % r][:, 0:n], T["QE%ds" % r][:, 0:n], "a%ds" % r, ["QE%d" % r], "LE%d" % r)
        if r == 2:
            shift_tops(2)
        else:
            fill(T.DB[:, 9:10], "DBz3", 1, 0.0)
        extract(r, 32, "KB", T.DB, "DB")
        upper_bases(r, T.DB, "DB", "DBz%d" % r)
        rows_of_bases(r)
        scatter_tops(r)
        lower(r, T.DB, "DB", T.sl[:, 16:16 + h], "tl")
        ts(T.SL[:, 0:h], "SL", T.sl[:, 16:16 + h], ["tl"], 1024.0, A.mult)
        scatter_links(r, T.SL[:, 0:h], "SL")
        mask_up()
        blend_list()
        if r == 2:
            lower(2, T.D2, "D2", T.tbB[:, 0:6], "tbB")
            ts(T.BL[:, 0:6], "BL", T.tbB[:, 0:6], ["tbB"], 1024.0, A.mult)
            tt(T.tbB[:, 0:6], "tbB", T.tbB[:, 0:6], T.KK[:, 18:24], ["tbB", "KK"], A.add)
            pump(f3)
        else:
            op("v", ["opc", "opf"], ["opc"], lambda: g.vector.tensor_copy(T.opc[:, 15:48:16], T.opc[:, 48:51]))
            op("v", ["opc", "CL3"], ["UP"], lambda: g.vector.tensor_copy(T.UP[:].indirect(T.CL3[:, b0:b0 + h]), T.opc[:, 0:48]))
            dma("y", T.op[:, :], T.UP[0:128:16, :], ["UP"], ["op"])
            quant(T.QVc[:], T.QVs[:], "QV", T.vb[:], ["vb"])
        layer(r, T["LE%dc" % r][:, 0:128], T["LE%ds" % r][:, 0:128], ["LE%d" % r, "LE%dz" % r], 128)
        blend(r)

    quant_x(4)
    for i, (a, n) in enumerate(CH[4]):
        mm(4 + i, n, T.QVc[:], T.QVs[:], T.QX4c[:, a:a + n], T.QX4s[:, a:a + n], ["QV", QK[4][i]])
    dma("s", T.oc[:, :], T.QX4c[:].bitcast(dt.uint8), QK[4], ["oc"])
    for k2 in range(4):
        dma("s" if k2 < 2 else "y", T.osc[4 * k2:4 * k2 + 4, :], T.QX4s[32 * k2:32 * k2 + 4, :], QK[4], ["osc%d" % k2])
    for i, (a, n) in enumerate(CH[4]):
        vcopy(T.ysb[:, a:a + n], "ysb%d" % i, T["p%d" % (4 + i)][:, 0:n], ["p%d" % (4 + i)])
        dma("y", T.y[:, a:a + n], T.ysb[:, a:a + n], ["ysb%d" % i], ["y%d" % i])

    for sem, val in cnt.items():
        if known["g"].get(sem, 0) < val:
            g.wait_ge(T.sem[sem], val)
